import numpy as np
import ml_dtypes


def mxq(x, axis, fmt="e4m3"):
    dtype, down = {"e4m3": (ml_dtypes.float8_e4m3fn, 7), "e5m2": (ml_dtypes.float8_e5m2, 14)}[fmt]
    v = np.moveaxis(np.asarray(x, np.float32).astype(ml_dtypes.bfloat16).astype(np.float64), axis, -1)
    blocks = v.reshape(v.shape[:-1] + (-1, 32))
    amax = np.abs(blocks).max(-1, keepdims=True)
    byte = np.maximum(np.where(amax > 0, np.frexp(amax)[1] - 1 + 127, 0) - down, 1)
    scale = np.exp2(byte - 127.0)
    codes = (blocks / scale).astype(np.float32).astype(dtype).astype(np.float64)
    return np.moveaxis((codes * scale).reshape(v.shape), -1, axis)


WIDE = False


def mx_kscale(k):
    if not WIDE:
        return np.ones(k)
    levels = np.array([10, -10, 5, -5, 0])
    if k % 512:
        return np.exp2(np.random.permutation(np.resize(levels, k // 32))).repeat(32)
    a = np.empty((k // 512, 16))
    for p in range(k // 512):
        a[p, :8] = np.random.permutation(np.resize(levels, 8))
        for g in range(8):
            far = levels[np.abs(levels - a[p, g]) >= 10]
            a[p, g + 8] = far[np.random.randint(len(far))]
    return np.exp2(a.ravel()).repeat(32)


def f64(x):
    return np.asarray(x).astype(np.float64)


def striped(idx):
    return np.tile(np.asarray(idx).reshape(-1, 16).T, (8, 1)).astype(np.uint16)


def unstriped(offs):
    return offs[:16].T.reshape(-1).astype(np.int64)


def striped8(idx):
    return np.asarray(idx).reshape(8, -1, 16).transpose(0, 2, 1).reshape(128, -1).astype(np.uint16)


def unstriped8(offs):
    return offs.reshape(8, 16, -1).transpose(0, 2, 1).reshape(8, -1).astype(np.int64)


def pick8(x, idx, run):
    r = np.arange(len(x))
    return x[r[:, None], idx[r % (8 * run) // run]]


E2M1 = np.array([0.0, 0.5, 1.0, 1.5, 2.0, 3.0, 4.0, 6.0, -0.0, -0.5, -1.0, -1.5, -2.0, -3.0, -4.0, -6.0])


def pack_weight(w, fmt):
    k, n = w.shape
    w = f64(np.asarray(w, np.float32).astype(ml_dtypes.bfloat16)).reshape(k // 32, 32, n)
    amax = np.abs(w).max(1)
    if fmt == "e4m3":
        byte = np.frexp(amax)[1] - 1 + 127 - 7
    else:
        mant, ex = np.frexp(amax / 6.0)
        byte = np.where(mant > 0.5, ex, ex - 1) + 127
    byte = np.clip(np.where(amax > 0, byte, 1), 1, 254)
    scaled = (w * np.exp2(127.0 - byte)[:, None, :]).reshape(k, n).astype(np.float32)
    by_word = np.ascontiguousarray(scaled.reshape(k // 512, 128, 4, n).transpose(0, 1, 3, 2))
    if fmt == "e4m3":
        words = by_word.astype(ml_dtypes.float8_e4m3fn).view(np.uint8)
    else:
        c = by_word.astype(ml_dtypes.float4_e2m1fn).view(np.uint8) & 0xF
        words = (c[..., 0::2] | (c[..., 1::2] << 4)).reshape(k // 512, 128, 2 * n)
    return np.ascontiguousarray(words), np.ascontiguousarray(byte.astype(np.uint8).reshape(k // 512, 16, n))


def unpack_weight(words, scales, fmt):
    g, _, n = scales.shape
    words = np.ascontiguousarray(words).reshape(g, 128, n, -1)
    if fmt == "e4m3":
        vals = words.view(ml_dtypes.float8_e4m3fn).astype(np.float64)
    else:
        nib = np.empty((g, 128, n, 4), np.uint8)
        nib[..., 0::2] = words & 0xF
        nib[..., 1::2] = words >> 4
        vals = E2M1[nib]
    vals = vals * np.repeat(np.exp2(scales.astype(np.float64) - 127.0), 8, axis=1)[..., None]
    return vals.transpose(0, 1, 3, 2).reshape(g * 512, n)


K, J, R, T, Z, M, C, O, N = 512, 512, 512, 2048, 512, 1024, 1024, 256, 256


def setup_inputs():
    n = np.random.standard_normal
    idx = np.random.permutation(T)[:J]
    idx2 = np.random.permutation(M)[:J]
    idx3 = np.stack([np.random.permutation(C)[:J] for _ in range(8)])
    idx4 = np.stack([np.random.permutation(C)[:J] for _ in range(8)])
    idx5 = np.stack([np.random.permutation(C)[:O] for _ in range(8)])
    idx6 = np.stack([np.random.permutation(C)[:O] for _ in range(8)])
    fk = mx_kscale(K)
    fr = mx_kscale(R)
    fz = mx_kscale(Z)
    xtp = pack_weight(n((K, T)) * fk[:, None], "e4m3")
    wp = pack_weight(n((K, R)) * 1 / np.sqrt(K) / fk[:, None] * fr, "e2m1")
    xop = pack_weight(n((Z, M)) / fz[:, None], "e2m1")
    w2p = pack_weight(n((Z, R)) * 1 / np.sqrt(Z) * fz[:, None] * fr, "e4m3")
    wbp = pack_weight(n((R, N)) * 1 / np.sqrt(R) / fr[:, None], "e4m3")
    return {
        "xt_words": xtp[0],
        "xt_scales": xtp[1],
        "w_words": wp[0],
        "w_scales": wp[1],
        "xo_words": xop[0],
        "xo_scales": xop[1],
        "w2_words": w2p[0],
        "w2_scales": w2p[1],
        "sa": (np.random.uniform(0.5, 1.6, (R, 1))).astype(np.float32),
        "sb": (np.random.uniform(0.5, 1.6, (R, 1))).astype(np.float32),
        "wb_words": wbp[0],
        "wb_scales": wbp[1],
        "offs": striped(idx),
        "offs2": striped(idx2),
        "offs3": striped8(idx3),
        "offs4": striped8(idx4),
        "offs5": striped8(idx5),
        "offs6": striped8(idx6),
    }


def reference(xt_words, xt_scales, w_words, w_scales, xo_words, xo_scales, w2_words, w2_scales, sa, sb, wb_words, wb_scales, offs, offs2, offs3, offs4, offs5, offs6):
    idx = unstriped(offs)
    idx2 = unstriped(offs2)
    idx3 = unstriped8(offs3)
    idx4 = unstriped8(offs4)
    idx5 = unstriped8(offs5)
    idx6 = unstriped8(offs6)
    xtu = unpack_weight(xt_words, xt_scales, "e4m3")
    wu = unpack_weight(w_words, w_scales, "e2m1")
    xou = unpack_weight(xo_words, xo_scales, "e2m1")
    w2u = unpack_weight(w2_words, w2_scales, "e4m3")
    wbu = unpack_weight(wb_words, wb_scales, "e4m3")
    xtidxg = xtu[:, idx]
    a = wu.T @ xtidxg
    xoidx2g = xou[:, idx2]
    b = w2u.T @ xoidx2g
    pw = np.zeros((R, C))
    pw[np.arange(R)[:, None], idx3[np.arange(R) % 512 // 64]] = a
    pv = np.zeros((R, C))
    pv[np.arange(R)[:, None], idx4[np.arange(R) % 512 // 64]] = b
    g1 = np.pad(pv, ((0, 0), (1, 0)))[:, :C]
    ph = np.maximum(pw, g1)
    g2 = np.pad(pw, ((0, 0), (1, 0)))[:, :C]
    pl = np.minimum(pv, g2)
    hid = pick8(ph, idx5, 64) * f64(sa) - pick8(pl, idx6, 64) * f64(sb)
    hidq = mxq(hid, 0, "e4m3")
    y = wbu.T @ hidq
    return y

@@ -1,0 +1,217 @@
+from contextlib import ExitStack
+
+import concourse.mybir as mybir
+
+K, J, R, T, Z, M, C, O, N = 512, 512, 512, 2048, 512, 1024, 1024, 256, 256
+FLOPS = 2 * K * R * J + 2 * Z * R * J + 2 * R * N * O
+
+F32 = mybir.dt.float32
+BF16 = mybir.dt.bfloat16
+I32 = mybir.dt.int32
+U32 = mybir.dt.uint32
+U16 = mybir.dt.uint16
+U8 = mybir.dt.uint8
+FP8X4 = mybir.dt.float8_e4m3fn_x4
+FP4X4 = mybir.dt.float4_e2m1fn_x4
+ALU = mybir.AluOpType
+COPY = mybir.ActivationFunctionType.Copy
+
+P = 128
+PACK = 4
+LIST_ROWS = 16
+
+
+def tile_picked_tokens_plain_two_staggered_one_plain_kernel(
+    tc, xt_words, xt_scales, w_words, w_scales, xo_words, xo_scales, w2_words, w2_scales,
+    sa, sb, wb_words, wb_scales, offs, offs2, offs3, offs4, offs5, offs6, out,
+):
+    nc = tc.nc
+    with ExitStack() as ctx:
+        keep = ctx.enter_context(tc.tile_pool(name="keep", bufs=1))
+        psum = ctx.enter_context(tc.psum_pool(name="psum", bufs=8))
+
+        def load_list(src, name):
+            lst = keep.tile([P, src.shape[1]], U16, name=name)
+            nc.sync.dma_start(lst[:], src)
+            return lst
+
+        def zero_plane(width, name):
+            plane = keep.tile([P, width], U8, name=name, align_bytes=64)
+            nc.vector.memset(plane[:].bitcast(I32), 0)
+            return plane
+
+        def load_plane(plane, scales):
+            for q in range(4):
+                nc.sync.dma_start(
+                    plane[32 * q : 32 * q + 4, :].bitcast(I32), scales[0, 4 * q : 4 * q + 4, :].bitcast(I32)
+                )
+
+        def load_staged(scales, name, queue):
+            width = scales.shape[2]
+            stage = keep.tile([4, 4, width // 4], I32, name=name)
+            queue.dma_start(stage[:], scales[0].bitcast(I32).rearrange("(q i) n -> i q n", i=4))
+            return stage
+
+        def spread(plane, stage):
+            for q in range(4):
+                nc.vector.tensor_copy(plane[32 * q : 32 * q + 4, :].bitcast(I32), stage[:, q, :])
+
+        def load_words(src, width, dtype, name, queue):
+            words = keep.tile([P, width], dtype, name=name, align_bytes=64)
+            queue.dma_start(words[:].bitcast(I32), src.bitcast(I32))
+            return words
+
+        def new_board(name, tag):
+            board = keep.tile([P, C], F32, name=name, tag=tag, align_bytes=64)
+            nc.vector.memset(board[:].bitcast(I32), 0)
+            return board
+
+        def entries(lst, lo, hi):
+            return lst[:, lo // LIST_ROWS : hi // LIST_ROWS]
+
+        xo_stage = load_staged(xo_scales, "xo_stage", nc.sync)
+        w2_stage = load_staged(w2_scales, "w2_stage", nc.scalar)
+        list2 = load_list(offs2, "list2")
+        xo_sb = load_words(xo_words[0], M, U16, "xo_sb", nc.sync)
+        w2_sb = load_words(w2_words[0].rearrange("p n t -> p (n t)"), R, U32, "w2_sb", nc.scalar)
+        list4 = load_list(offs4, "list4")
+        xo_plane = zero_plane(M, "xo_plane")
+        w2_plane = zero_plane(R, "w2_plane")
+        pv = [new_board("pv0", "pv0")]
+        xt_plane = zero_plane(T, "xt_plane")
+        w_plane = zero_plane(R, "w_plane")
+        wb_plane = zero_plane(N, "wb_plane")
+
+        w2_dealt = [keep.tile([P, P], U32, name="w2_dealt%d" % t, align_bytes=64) for t in range(PACK)]
+        w2_dealt_sc = [keep.tile([P, P], U8, name="w2_dealt_sc%d" % t, align_bytes=64) for t in range(PACK)]
+        xo_g = keep.tile([P, J], U16, name="xo_g", align_bytes=64)
+        xo_g_sc = keep.tile([P, J], U8, name="xo_g_sc", align_bytes=64)
+        b_sb = [keep.tile([P, J], F32, name="b_sb%d" % t) for t in range(PACK)]
+
+        def gather_xo_scales(lo, hi):
+            nc.vector.tensor_copy(xo_g_sc[:, lo:hi], xo_plane[:].indirect(entries(list2, lo, hi)))
+
+        def gather_xo_words(lo, hi):
+            nc.vector.tensor_copy(xo_g[:, lo:hi], xo_sb[:].indirect(entries(list2, lo, hi)))
+
+        def product_b(t, lo, hi, copy_out):
+            acc = psum.tile([P, J], F32, name="acc")
+            nc.tensor.matmul_mx(
+                out=acc[:, : hi - lo], lhsT=w2_dealt[t][:].bitcast(FP8X4), lhsT_scale=w2_dealt_sc[t][:],
+                rhs=xo_g[:, lo:hi].bitcast(FP4X4), rhs_scale=xo_g_sc[:, lo:hi], start=True, stop=True,
+            )
+            copy_out(b_sb[t][:, lo:hi], acc[:, : hi - lo])
+
+        def scatter_b(t, lo, hi):
+            nc.scalar.activation(pv[t][:].indirect(entries(list4, lo, hi)), b_sb[t][:, lo:hi], COPY)
+
+        spread(xo_plane, xo_stage)
+        gather_xo_scales(0, 256)
+        spread(w2_plane, w2_stage)
+        for t in range(PACK):
+            nc.scalar.copy(w2_dealt[t][:], w2_sb[:, t:R:PACK])
+        nc.vector.tensor_copy(w2_dealt_sc[0][:], w2_plane[:, 0:R:PACK])
+        gather_xo_words(0, 128)
+        product_b(0, 0, 128, nc.scalar.copy)
+        scatter_b(0, 0, 128)
+        gather_xo_words(128, 256)
+        product_b(0, 128, 256, nc.vector.tensor_copy)
+        scatter_b(0, 128, 256)
+        gather_xo_scales(256, 512)
+        gather_xo_words(256, 512)
+        product_b(0, 256, 512, nc.vector.tensor_copy)
+        scatter_b(0, 256, 512)
+        for t in range(1, PACK):
+            nc.vector.tensor_copy(w2_dealt_sc[t][:], w2_plane[:, t:R:PACK])
+        for t in range(1, PACK):
+            pv.append(new_board("pv%d" % t, "w2_dealt%d" % (t - 1)))
+            product_b(t, 0, J, nc.vector.tensor_copy)
+            scatter_b(t, 0, J)
+
+        list1 = load_list(offs, "list1")
+        load_plane(xt_plane, xt_scales)
+        load_plane(w_plane, w_scales)
+        xt_sb = load_words(xt_words[0].rearrange("p n t -> p (n t)"), T, U32, "xt_sb", nc.sync)
+        w_sb = load_words(w_words[0], 2 * R, U8, "w_sb", nc.sync)
+        list3 = load_list(offs3, "list3")
+
+        xt_g = keep.tile([P, J], U32, name="xt_g", align_bytes=64)
+        xt_g_sc = keep.tile([P, J], U8, name="xt_g_sc", align_bytes=64)
+        nc.vector.tensor_copy(xt_g_sc[:], xt_plane[:].indirect(list1[:]))
+        nc.vector.tensor_copy(xt_g[:], xt_sb[:].indirect(list1[:]))
+        w_dealt = keep.tile([P, PACK, P, 2], U8, name="w_dealt", align_bytes=64)
+        w_dealt_sc = keep.tile([P, PACK, P], U8, name="w_dealt_sc", align_bytes=64)
+        nc.vector.tensor_copy(w_dealt[:], w_sb[:].rearrange("p (m t h) -> p t m h", t=PACK, h=2))
+        nc.vector.tensor_copy(w_dealt_sc[:], w_plane[:].rearrange("p (m t) -> p t m", t=PACK))
+
+        pw = []
+        for t in range(PACK):
+            pw.append(new_board("pw%d" % t, "w2_dealt3" if t == 0 else "w2_dealt_sc%d" % t))
+            acc = psum.tile([P, J], F32, name="acc")
+            nc.tensor.matmul_mx(
+                out=acc[:], lhsT=w_dealt[:, t, :, :].rearrange("p m h -> p (m h)").bitcast(FP4X4),
+                lhsT_scale=w_dealt_sc[:, t, :], rhs=xt_g[:].bitcast(FP8X4), rhs_scale=xt_g_sc[:],
+                start=True, stop=True,
+            )
+            a_sb = keep.tile([P, J], F32, name="a_sb%d" % t)
+            nc.vector.tensor_copy(a_sb[:], acc[:])
+            nc.scalar.activation(pw[t][:].indirect(list3[:]), a_sb[:], COPY)
+
+        list5 = load_list(offs5, "list5")
+        list6 = load_list(offs6, "list6")
+        sa_sb = keep.tile([P, PACK], F32, name="sa_sb")
+        sb_sb = keep.tile([P, PACK], F32, name="sb_sb")
+        nc.sync.dma_start(sa_sb[:], sa.rearrange("(p t) o -> p (t o)", t=PACK))
+        nc.sync.dma_start(sb_sb[:], sb.rearrange("(p t) o -> p (t o)", t=PACK))
+        load_plane(wb_plane, wb_scales)
+        wb_sb = load_words(wb_words[0].rearrange("p n t -> p (n t)"), N, U32, "wb_sb", nc.sync)
+
+        ph, pl = [], []
+        for t in range(PACK):
+            upper = keep.tile([P, C], F32, name="ph%d" % t)
+            lower = keep.tile([P, C], F32, name="pl%d" % t)
+            nc.vector.tensor_scalar_max(upper[:, 0:1], pw[t][:, 0:1], 0.0)
+            nc.vector.tensor_tensor(upper[:, 1:C], pw[t][:, 1:C], pv[t][:, 0 : C - 1], ALU.max)
+            nc.vector.tensor_scalar_min(lower[:, 0:1], pv[t][:, 0:1], 0.0)
+            nc.vector.tensor_tensor(lower[:, 1:C], pv[t][:, 1:C], pw[t][:, 0 : C - 1], ALU.min)
+            ph.append(upper)
+            pl.append(lower)
+
+        halves = (slice(0, O // 2), slice(O // 2, O))
+        hid = keep.tile([P, PACK, O], BF16, name="hid")
+        for t in range(PACK):
+            hi_part = keep.tile([P, O], F32, name="hi_part%d" % t)
+            lo_part = keep.tile([P, O], F32, name="lo_part%d" % t)
+            nc.scalar.activation(hi_part[:], ph[t][:].indirect(list5[:]), COPY, scale=sa_sb[:, t : t + 1])
+            nc.scalar.activation(lo_part[:], pl[t][:].indirect(list6[:]), COPY, scale=sb_sb[:, t : t + 1])
+            for cols in halves if t == PACK - 1 else (slice(0, O),):
+                nc.vector.tensor_tensor(hid[:, t, cols], hi_part[:, cols], lo_part[:, cols], ALU.subtract)
+
+        grouped, hid_q, hid_sc = [], [], []
+        for h, cols in enumerate(halves):
+            grouped.append(keep.tile([P, O // 2, PACK], BF16, name="grouped%d" % h, align_bytes=64))
+            nc.vector.tensor_copy(grouped[h][:], hid[:, :, cols].rearrange("p t o -> p o t"))
+        for h, cols in enumerate(halves):
+            hid_q.append(keep.tile([P, O // 2], U32, name="hid_q%d" % h, align_bytes=64))
+            hid_sc.append(keep.tile([P, O // 2], U8, name="hid_sc%d" % h, align_bytes=64))
+            nc.vector.quantize_mx(
+                out=hid_q[h][:].bitcast(FP8X4), scales=hid_sc[h][:], in_=grouped[h][:].rearrange("p o t -> p (o t)")
+            )
+
+        def product_y(acc_cols, u, h):
+            nc.tensor.matmul_mx(
+                out=acc_cols, lhsT=wb_sb[:, u * P : (u + 1) * P].bitcast(FP8X4),
+                lhsT_scale=wb_plane[:, u * P : (u + 1) * P], rhs=hid_q[h][:].bitcast(FP8X4), rhs_scale=hid_sc[h][:],
+                start=True, stop=True,
+            )
+
+        res = keep.tile([P, N // P, O], F32, name="res")
+        acc = psum.tile([P, N // P, O // 2], F32, name="acc")
+        for u in range(N // P):
+            product_y(acc[:, u, :], u, 0)
+        nc.scalar.copy(res[:, :, halves[0]], acc[:])
+        for u, (copy_out, queue) in enumerate(((nc.vector.tensor_copy, nc.sync), (nc.scalar.copy, nc.scalar))):
+            acc = psum.tile([P, O // 2], F32, name="acc")
+            product_y(acc[:], u, 1)
+            copy_out(res[:, u, halves[1]], acc[:])
+            queue.dma_start(out[u * P : (u + 1) * P, :], res[:, u, :])

@@ -19,6 +19,7 @@ COPY = mybir.ActivationFunctionType.Copy
 P = 128
 PACK = 4
 LIST_ROWS = 16
+SPARE = 8
 
 
 def tile_picked_tokens_plain_two_staggered_one_plain_kernel(
@@ -35,8 +36,8 @@ def tile_picked_tokens_plain_two_staggered_one_plain_kernel(
             nc.sync.dma_start(lst[:], src)
             return lst
 
-        def zero_plane(width, name):
-            plane = keep.tile([P, width], U8, name=name, align_bytes=64)
+        def zero_plane(width, name, tag):
+            plane = keep.tile([P, width], U8, name=name, tag=tag, align_bytes=64)
             nc.vector.memset(plane[:].bitcast(I32), 0)
             return plane
 
@@ -62,25 +63,22 @@ def tile_picked_tokens_plain_two_staggered_one_plain_kernel(
             return words
 
         def new_board(name, tag):
-            board = keep.tile([P, C], F32, name=name, tag=tag, align_bytes=64)
+            board = keep.tile([P, C + SPARE], F32, name=name, tag=tag, align_bytes=64)
             nc.vector.memset(board[:].bitcast(I32), 0)
             return board
 
         def entries(lst, lo, hi):
             return lst[:, lo // LIST_ROWS : hi // LIST_ROWS]
 
-        xo_stage = load_staged(xo_scales, "xo_stage", nc.sync)
+        xo_plane = zero_plane(M, "xo_plane", "xo_plane")
         w2_stage = load_staged(w2_scales, "w2_stage", nc.scalar)
         list2 = load_list(offs2, "list2")
         xo_sb = load_words(xo_words[0], M, U16, "xo_sb", nc.sync)
         w2_sb = load_words(w2_words[0].rearrange("p n t -> p (n t)"), R, U32, "w2_sb", nc.scalar)
+        load_plane(xo_plane, xo_scales)
         list4 = load_list(offs4, "list4")
-        xo_plane = zero_plane(M, "xo_plane")
-        w2_plane = zero_plane(R, "w2_plane")
-        pv = [new_board("pv0", "pv0")]
-        xt_plane = zero_plane(T, "xt_plane")
-        w_plane = zero_plane(R, "w_plane")
-        wb_plane = zero_plane(N, "wb_plane")
+        w2_plane = zero_plane(R, "w2_plane", "w2_plane")
+        pv = [new_board("pv0", "pv0"), new_board("pv1", "pv1")]
 
         w2_dealt = [keep.tile([P, P], U32, name="w2_dealt%d" % t, align_bytes=64) for t in range(PACK)]
         w2_dealt_sc = [keep.tile([P, P], U8, name="w2_dealt_sc%d" % t, align_bytes=64) for t in range(PACK)]
@@ -105,26 +103,23 @@ def tile_picked_tokens_plain_two_staggered_one_plain_kernel(
         def scatter_b(t, lo, hi):
             nc.scalar.activation(pv[t][:].indirect(entries(list4, lo, hi)), b_sb[t][:, lo:hi], COPY)
 
-        spread(xo_plane, xo_stage)
-        gather_xo_scales(0, 256)
         spread(w2_plane, w2_stage)
         for t in range(PACK):
             nc.scalar.copy(w2_dealt[t][:], w2_sb[:, t:R:PACK])
         nc.vector.tensor_copy(w2_dealt_sc[0][:], w2_plane[:, 0:R:PACK])
-        gather_xo_words(0, 128)
-        product_b(0, 0, 128, nc.scalar.copy)
-        scatter_b(0, 0, 128)
-        gather_xo_words(128, 256)
-        product_b(0, 128, 256, nc.vector.tensor_copy)
-        scatter_b(0, 128, 256)
-        gather_xo_scales(256, 512)
-        gather_xo_words(256, 512)
-        product_b(0, 256, 512, nc.vector.tensor_copy)
-        scatter_b(0, 256, 512)
-        for t in range(1, PACK):
+        for lo, hi in ((0, 128), (128, 256), (256, 512)):
+            gather_xo_words(lo, hi)
+            gather_xo_scales(lo, hi)
+            if lo == 0:
+                nc.vector.tensor_copy(w2_dealt_sc[1][:], w2_plane[:, 1:R:PACK])
+            for t in range(2):
+                product_b(t, lo, hi, nc.scalar.copy if (lo, t) == (0, 0) else nc.vector.tensor_copy)
+                scatter_b(t, lo, hi)
+        xt_plane = zero_plane(T, "xt_plane", "w2_dealt_sc0")
+        w_plane = zero_plane(R, "w_plane", "w2_dealt_sc1")
+        for t in range(2, PACK):
             nc.vector.tensor_copy(w2_dealt_sc[t][:], w2_plane[:, t:R:PACK])
-        for t in range(1, PACK):
-            pv.append(new_board("pv%d" % t, "w2_dealt%d" % (t - 1)))
+            pv.append(new_board("pv%d" % t, "w2_dealt%d" % (t - 2)))
             product_b(t, 0, J, nc.vector.tensor_copy)
             scatter_b(t, 0, J)
 
@@ -146,7 +141,7 @@ def tile_picked_tokens_plain_two_staggered_one_plain_kernel(
 
         pw = []
         for t in range(PACK):
-            pw.append(new_board("pw%d" % t, "w2_dealt3" if t == 0 else "w2_dealt_sc%d" % t))
+            pw.append(new_board("pw%d" % t, ("w2_dealt2", "w_sb", "w2_dealt_sc1", "xt_sb")[t]))
             acc = psum.tile([P, J], F32, name="acc")
             nc.tensor.matmul_mx(
                 out=acc[:], lhsT=w_dealt[:, t, :, :].rearrange("p m h -> p (m h)").bitcast(FP4X4),
@@ -163,6 +158,7 @@ def tile_picked_tokens_plain_two_staggered_one_plain_kernel(
         sb_sb = keep.tile([P, PACK], F32, name="sb_sb")
         nc.sync.dma_start(sa_sb[:], sa.rearrange("(p t) o -> p (t o)", t=PACK))
         nc.sync.dma_start(sb_sb[:], sb.rearrange("(p t) o -> p (t o)", t=PACK))
+        wb_plane = zero_plane(N, "wb_plane", "w2_dealt3")
         load_plane(wb_plane, wb_scales)
         wb_sb = load_words(wb_words[0].rearrange("p n t -> p (n t)"), N, U32, "wb_sb", nc.sync)
 
@@ -170,27 +166,29 @@ def tile_picked_tokens_plain_two_staggered_one_plain_kernel(
         for t in range(PACK):
             upper = keep.tile([P, C], F32, name="ph%d" % t)
             lower = keep.tile([P, C], F32, name="pl%d" % t)
-            nc.vector.tensor_scalar_max(upper[:, 0:1], pw[t][:, 0:1], 0.0)
+            nc.vector.tensor_tensor(upper[:, 0:1], pw[t][:, 0:1], pv[t][:, C : C + 1], ALU.max)
             nc.vector.tensor_tensor(upper[:, 1:C], pw[t][:, 1:C], pv[t][:, 0 : C - 1], ALU.max)
-            nc.vector.tensor_scalar_min(lower[:, 0:1], pv[t][:, 0:1], 0.0)
+            nc.vector.tensor_tensor(lower[:, 0:1], pv[t][:, 0:1], pw[t][:, C : C + 1], ALU.min)
             nc.vector.tensor_tensor(lower[:, 1:C], pv[t][:, 1:C], pw[t][:, 0 : C - 1], ALU.min)
             ph.append(upper)
             pl.append(lower)
 
         halves = (slice(0, O // 2), slice(O // 2, O))
-        hid = keep.tile([P, PACK, O], BF16, name="hid")
-        for t in range(PACK):
-            hi_part = keep.tile([P, O], F32, name="hi_part%d" % t)
-            lo_part = keep.tile([P, O], F32, name="lo_part%d" % t)
-            nc.scalar.activation(hi_part[:], ph[t][:].indirect(list5[:]), COPY, scale=sa_sb[:, t : t + 1])
-            nc.scalar.activation(lo_part[:], pl[t][:].indirect(list6[:]), COPY, scale=sb_sb[:, t : t + 1])
-            for cols in halves if t == PACK - 1 else (slice(0, O),):
-                nc.vector.tensor_tensor(hid[:, t, cols], hi_part[:, cols], lo_part[:, cols], ALU.subtract)
+        grouped = [keep.tile([P, O // 2, PACK], BF16, name="grouped%d" % h, align_bytes=64) for h in range(2)]
+        for pair in range(2):
+            hi_part = keep.tile([P, 2, O], F32, name="hi_part%d" % pair)
+            lo_part = keep.tile([P, 2, O], F32, name="lo_part%d" % pair)
+            for e in range(2):
+                t = 2 * pair + e
+                nc.scalar.activation(hi_part[:, e, :], ph[t][:].indirect(list5[:]), COPY, scale=sa_sb[:, t : t + 1])
+                nc.scalar.activation(lo_part[:, e, :], pl[t][:].indirect(list6[:]), COPY, scale=sb_sb[:, t : t + 1])
+            for h, cols in enumerate(halves):
+                nc.vector.tensor_tensor(
+                    grouped[h][:, :, 2 * pair : 2 * pair + 2], hi_part[:, :, cols].rearrange("p e o -> p o e"),
+                    lo_part[:, :, cols].rearrange("p e o -> p o e"), ALU.subtract,
+                )
 
-        grouped, hid_q, hid_sc = [], [], []
-        for h, cols in enumerate(halves):
-            grouped.append(keep.tile([P, O // 2, PACK], BF16, name="grouped%d" % h, align_bytes=64))
-            nc.vector.tensor_copy(grouped[h][:], hid[:, :, cols].rearrange("p t o -> p o t"))
+        hid_q, hid_sc = [], []
         for h, cols in enumerate(halves):
             hid_q.append(keep.tile([P, O // 2], U32, name="hid_q%d" % h, align_bytes=64))
             hid_sc.append(keep.tile([P, O // 2], U8, name="hid_sc%d" % h, align_bytes=64))
@@ -205,13 +203,15 @@ def tile_picked_tokens_plain_two_staggered_one_plain_kernel(
                 start=True, stop=True,
             )
 
-        res = keep.tile([P, N // P, O], F32, name="res")
+        res = keep.tile([P, N // P, O // 2], F32, name="res")
         acc = psum.tile([P, N // P, O // 2], F32, name="acc")
         for u in range(N // P):
             product_y(acc[:, u, :], u, 0)
-        nc.scalar.copy(res[:, :, halves[0]], acc[:])
+        nc.scalar.copy(res[:], acc[:])
+        nc.sync.dma_start(out[:, halves[0]].rearrange("(u p) o -> p u o", p=P), res[:])
         for u, (copy_out, queue) in enumerate(((nc.vector.tensor_copy, nc.sync), (nc.scalar.copy, nc.scalar))):
             acc = psum.tile([P, O // 2], F32, name="acc")
             product_y(acc[:], u, 1)
-            copy_out(res[:, u, halves[1]], acc[:])
-            queue.dma_start(out[u * P : (u + 1) * P, :], res[:, u, :])
+            last = keep.tile([P, O // 2], F32, name="last%d" % u)
+            copy_out(last[:], acc[:])
+            queue.dma_start(out[u * P : (u + 1) * P, halves[1]], last[:])

from contextlib import ExitStack

import concourse.mybir as mybir

K, J, R, T, Z, M, C, O, N = 512, 512, 512, 2048, 512, 1024, 1024, 256, 256
FLOPS = 2 * K * R * J + 2 * Z * R * J + 2 * R * N * O

F32 = mybir.dt.float32
BF16 = mybir.dt.bfloat16
I32 = mybir.dt.int32
U32 = mybir.dt.uint32
U16 = mybir.dt.uint16
U8 = mybir.dt.uint8
FP8X4 = mybir.dt.float8_e4m3fn_x4
FP4X4 = mybir.dt.float4_e2m1fn_x4
ALU = mybir.AluOpType
COPY = mybir.ActivationFunctionType.Copy

P = 128
PACK = 4
LIST_ROWS = 16
SPARE = 8


def tile_picked_tokens_plain_two_staggered_one_plain_kernel(
    tc, xt_words, xt_scales, w_words, w_scales, xo_words, xo_scales, w2_words, w2_scales,
    sa, sb, wb_words, wb_scales, offs, offs2, offs3, offs4, offs5, offs6, out,
):
    nc = tc.nc
    with ExitStack() as ctx:
        keep = ctx.enter_context(tc.tile_pool(name="keep", bufs=1))
        psum = ctx.enter_context(tc.psum_pool(name="psum", bufs=8))

        def load_list(src, name):
            lst = keep.tile([P, src.shape[1]], U16, name=name)
            nc.sync.dma_start(lst[:], src)
            return lst

        def zero_plane(width, name, tag):
            plane = keep.tile([P, width], U8, name=name, tag=tag, align_bytes=64)
            nc.vector.memset(plane[:].bitcast(I32), 0)
            return plane

        def load_plane(plane, scales):
            for q in range(4):
                nc.sync.dma_start(
                    plane[32 * q : 32 * q + 4, :].bitcast(I32), scales[0, 4 * q : 4 * q + 4, :].bitcast(I32)
                )

        def load_staged(scales, name, queue):
            width = scales.shape[2]
            stage = keep.tile([4, 4, width // 4], I32, name=name)
            queue.dma_start(stage[:], scales[0].bitcast(I32).rearrange("(q i) n -> i q n", i=4))
            return stage

        def spread(plane, stage):
            for q in range(4):
                nc.vector.tensor_copy(plane[32 * q : 32 * q + 4, :].bitcast(I32), stage[:, q, :])

        def load_words(src, width, dtype, name, queue):
            words = keep.tile([P, width], dtype, name=name, align_bytes=64)
            queue.dma_start(words[:].bitcast(I32), src.bitcast(I32))
            return words

        def new_board(name, tag):
            board = keep.tile([P, C + SPARE], F32, name=name, tag=tag, align_bytes=64)
            nc.vector.memset(board[:].bitcast(I32), 0)
            return board

        def entries(lst, lo, hi):
            return lst[:, lo // LIST_ROWS : hi // LIST_ROWS]

        xo_plane = zero_plane(M, "xo_plane", "xo_plane")
        w2_stage = load_staged(w2_scales, "w2_stage", nc.scalar)
        list2 = load_list(offs2, "list2")
        xo_sb = load_words(xo_words[0], M, U16, "xo_sb", nc.sync)
        w2_sb = load_words(w2_words[0].rearrange("p n t -> p (n t)"), R, U32, "w2_sb", nc.scalar)
        load_plane(xo_plane, xo_scales)
        list4 = load_list(offs4, "list4")
        w2_plane = zero_plane(R, "w2_plane", "w2_plane")
        pv = [new_board("pv0", "pv0"), new_board("pv1", "pv1")]

        w2_dealt = [keep.tile([P, P], U32, name="w2_dealt%d" % t, align_bytes=64) for t in range(PACK)]
        w2_dealt_sc = [keep.tile([P, P], U8, name="w2_dealt_sc%d" % t, align_bytes=64) for t in range(PACK)]
        xo_g = keep.tile([P, J], U16, name="xo_g", align_bytes=64)
        xo_g_sc = keep.tile([P, J], U8, name="xo_g_sc", align_bytes=64)
        b_sb = [keep.tile([P, J], F32, name="b_sb%d" % t) for t in range(PACK)]

        def gather_xo_scales(lo, hi):
            nc.vector.tensor_copy(xo_g_sc[:, lo:hi], xo_plane[:].indirect(entries(list2, lo, hi)))

        def gather_xo_words(lo, hi):
            nc.vector.tensor_copy(xo_g[:, lo:hi], xo_sb[:].indirect(entries(list2, lo, hi)))

        def product_b(t, lo, hi, copy_out):
            acc = psum.tile([P, J], F32, name="acc")
            nc.tensor.matmul_mx(
                out=acc[:, : hi - lo], lhsT=w2_dealt[t][:].bitcast(FP8X4), lhsT_scale=w2_dealt_sc[t][:],
                rhs=xo_g[:, lo:hi].bitcast(FP4X4), rhs_scale=xo_g_sc[:, lo:hi], start=True, stop=True,
            )
            copy_out(b_sb[t][:, lo:hi], acc[:, : hi - lo])

        def scatter_b(t, lo, hi):
            nc.scalar.activation(pv[t][:].indirect(entries(list4, lo, hi)), b_sb[t][:, lo:hi], COPY)

        spread(w2_plane, w2_stage)
        for t in range(PACK):
            nc.scalar.copy(w2_dealt[t][:], w2_sb[:, t:R:PACK])
        nc.vector.tensor_copy(w2_dealt_sc[0][:], w2_plane[:, 0:R:PACK])
        for lo, hi in ((0, 128), (128, 256), (256, 512)):
            gather_xo_words(lo, hi)
            gather_xo_scales(lo, hi)
            if lo == 0:
                nc.vector.tensor_copy(w2_dealt_sc[1][:], w2_plane[:, 1:R:PACK])
            for t in range(2):
                product_b(t, lo, hi, nc.scalar.copy if (lo, t) == (0, 0) else nc.vector.tensor_copy)
                scatter_b(t, lo, hi)
        xt_plane = zero_plane(T, "xt_plane", "w2_dealt_sc0")
        w_plane = zero_plane(R, "w_plane", "w2_dealt_sc1")
        for t in range(2, PACK):
            nc.vector.tensor_copy(w2_dealt_sc[t][:], w2_plane[:, t:R:PACK])
            pv.append(new_board("pv%d" % t, "w2_dealt%d" % (t - 2)))
            product_b(t, 0, J, nc.vector.tensor_copy)
            scatter_b(t, 0, J)

        list1 = load_list(offs, "list1")
        load_plane(xt_plane, xt_scales)
        load_plane(w_plane, w_scales)
        xt_sb = load_words(xt_words[0].rearrange("p n t -> p (n t)"), T, U32, "xt_sb", nc.sync)
        w_sb = load_words(w_words[0], 2 * R, U8, "w_sb", nc.sync)
        list3 = load_list(offs3, "list3")

        xt_g = keep.tile([P, J], U32, name="xt_g", align_bytes=64)
        xt_g_sc = keep.tile([P, J], U8, name="xt_g_sc", align_bytes=64)
        nc.vector.tensor_copy(xt_g_sc[:], xt_plane[:].indirect(list1[:]))
        nc.vector.tensor_copy(xt_g[:], xt_sb[:].indirect(list1[:]))
        w_dealt = keep.tile([P, PACK, P, 2], U8, name="w_dealt", align_bytes=64)
        w_dealt_sc = keep.tile([P, PACK, P], U8, name="w_dealt_sc", align_bytes=64)
        nc.vector.tensor_copy(w_dealt[:], w_sb[:].rearrange("p (m t h) -> p t m h", t=PACK, h=2))
        nc.vector.tensor_copy(w_dealt_sc[:], w_plane[:].rearrange("p (m t) -> p t m", t=PACK))

        pw = []
        for t in range(PACK):
            pw.append(new_board("pw%d" % t, ("w2_dealt2", "w_sb", "w2_dealt_sc1", "xt_sb")[t]))
            acc = psum.tile([P, J], F32, name="acc")
            nc.tensor.matmul_mx(
                out=acc[:], lhsT=w_dealt[:, t, :, :].rearrange("p m h -> p (m h)").bitcast(FP4X4),
                lhsT_scale=w_dealt_sc[:, t, :], rhs=xt_g[:].bitcast(FP8X4), rhs_scale=xt_g_sc[:],
                start=True, stop=True,
            )
            a_sb = keep.tile([P, J], F32, name="a_sb%d" % t)
            nc.vector.tensor_copy(a_sb[:], acc[:])
            nc.scalar.activation(pw[t][:].indirect(list3[:]), a_sb[:], COPY)

        list5 = load_list(offs5, "list5")
        list6 = load_list(offs6, "list6")
        sa_sb = keep.tile([P, PACK], F32, name="sa_sb")
        sb_sb = keep.tile([P, PACK], F32, name="sb_sb")
        nc.sync.dma_start(sa_sb[:], sa.rearrange("(p t) o -> p (t o)", t=PACK))
        nc.sync.dma_start(sb_sb[:], sb.rearrange("(p t) o -> p (t o)", t=PACK))
        wb_plane = zero_plane(N, "wb_plane", "w2_dealt3")
        load_plane(wb_plane, wb_scales)
        wb_sb = load_words(wb_words[0].rearrange("p n t -> p (n t)"), N, U32, "wb_sb", nc.sync)

        ph, pl = [], []
        for t in range(PACK):
            upper = keep.tile([P, C], F32, name="ph%d" % t)
            lower = keep.tile([P, C], F32, name="pl%d" % t)
            nc.vector.tensor_tensor(upper[:, 0:1], pw[t][:, 0:1], pv[t][:, C : C + 1], ALU.max)
            nc.vector.tensor_tensor(upper[:, 1:C], pw[t][:, 1:C], pv[t][:, 0 : C - 1], ALU.max)
            nc.vector.tensor_tensor(lower[:, 0:1], pv[t][:, 0:1], pw[t][:, C : C + 1], ALU.min)
            nc.vector.tensor_tensor(lower[:, 1:C], pv[t][:, 1:C], pw[t][:, 0 : C - 1], ALU.min)
            ph.append(upper)
            pl.append(lower)

        halves = (slice(0, O // 2), slice(O // 2, O))
        grouped = [keep.tile([P, O // 2, PACK], BF16, name="grouped%d" % h, align_bytes=64) for h in range(2)]
        for pair in range(2):
            hi_part = keep.tile([P, 2, O], F32, name="hi_part%d" % pair)
            lo_part = keep.tile([P, 2, O], F32, name="lo_part%d" % pair)
            for e in range(2):
                t = 2 * pair + e
                nc.scalar.activation(hi_part[:, e, :], ph[t][:].indirect(list5[:]), COPY, scale=sa_sb[:, t : t + 1])
                nc.scalar.activation(lo_part[:, e, :], pl[t][:].indirect(list6[:]), COPY, scale=sb_sb[:, t : t + 1])
            for h, cols in enumerate(halves):
                nc.vector.tensor_tensor(
                    grouped[h][:, :, 2 * pair : 2 * pair + 2], hi_part[:, :, cols].rearrange("p e o -> p o e"),
                    lo_part[:, :, cols].rearrange("p e o -> p o e"), ALU.subtract,
                )

        hid_q, hid_sc = [], []
        for h, cols in enumerate(halves):
            hid_q.append(keep.tile([P, O // 2], U32, name="hid_q%d" % h, align_bytes=64))
            hid_sc.append(keep.tile([P, O // 2], U8, name="hid_sc%d" % h, align_bytes=64))
            nc.vector.quantize_mx(
                out=hid_q[h][:].bitcast(FP8X4), scales=hid_sc[h][:], in_=grouped[h][:].rearrange("p o t -> p (o t)")
            )

        def product_y(acc_cols, u, h):
            nc.tensor.matmul_mx(
                out=acc_cols, lhsT=wb_sb[:, u * P : (u + 1) * P].bitcast(FP8X4),
                lhsT_scale=wb_plane[:, u * P : (u + 1) * P], rhs=hid_q[h][:].bitcast(FP8X4), rhs_scale=hid_sc[h][:],
                start=True, stop=True,
            )

        res = keep.tile([P, N // P, O // 2], F32, name="res")
        acc = psum.tile([P, N // P, O // 2], F32, name="acc")
        for u in range(N // P):
            product_y(acc[:, u, :], u, 0)
        nc.scalar.copy(res[:], acc[:])
        nc.sync.dma_start(out[:, halves[0]].rearrange("(u p) o -> p u o", p=P), res[:])
        for u, (copy_out, queue) in enumerate(((nc.vector.tensor_copy, nc.sync), (nc.scalar.copy, nc.scalar))):
            acc = psum.tile([P, O // 2], F32, name="acc")
            product_y(acc[:], u, 1)
            last = keep.tile([P, O // 2], F32, name="last%d" % u)
            copy_out(last[:], acc[:])
            queue.dma_start(out[u * P : (u + 1) * P, halves[1]], last[:])
